import numpy as np, ml_dtypes
CORES = [76,84,92,100,108,116,124]
N = 7
KB, QP = 1, 32
WB = 1
def setup_inputs(rng):
    q = rng.standard_normal((N, 128, QP), dtype=np.float32) / 4; k = rng.standard_normal((N, 128, KB * 128), dtype=np.float32)
    a = 2 * np.pi * rng.random((N, QP)); s = 400 * rng.random((N, QP)) ** 1.5; q[:, 0, :] = s * np.cos(a); q[:, 1, :] = s * np.sin(a); q[:, 2, :] = 150 * rng.standard_normal((N, QP)); k[:, 2, :] = 1 + k[:, 2, :] / 50
    a = (2 * np.pi * rng.random() + np.pi / 2 * (rng.permutation(N).reshape(N, 1, 1) + 0.5) / N - 0.5 + (np.arange(KB).reshape(1, KB, 1) + rng.random((N, KB, 128))) / KB).reshape(N, KB * 128); k[:, 0, :] = np.cos(a); k[:, 1, :] = np.sin(a)
    return {"q": q.astype(ml_dtypes.bfloat16), "k": k.astype(ml_dtypes.bfloat16), "v": rng.standard_normal((N, 128, KB * 128), dtype=np.float32).astype(ml_dtypes.bfloat16)}
def setup_inputs_big(rng):
    d = setup_inputs(rng)
    for k in ("v",): d[k] = (d[k].astype(np.float32) * 1048576.0).astype(d[k].dtype)
    return d
def setup_inputs_small(rng):
    d = setup_inputs(rng)
    for k in ("v",): d[k] = (d[k].astype(np.float32) * (1 / 1048576.0)).astype(d[k].dtype)
    return d
def reference(q, k, v):
    Q, K, V = q.astype(np.float64), k.astype(np.float64), v.astype(np.float64)
    y = np.zeros((N, QP, 128))
    for r in range(N):
        js = list(range(max(0, r - WB), r + 1))
        S = np.concatenate([K[j].T @ Q[r] for j in js], axis=0)
        P = np.exp(S - S.max(axis=0)); P = P / P.sum(axis=0)
        y[r] = P.T @ np.concatenate([V[j][:, 128 * b:128 * b + 128] for j in js for b in range(KB)], axis=0)
    return {"y": y.astype(ml_dtypes.bfloat16)}

@@ -1,0 +1,170 @@
+from concourse.mybir import AluOpType, AxisListType, ActivationFunctionType
+
+BF, F32 = "bfloat16", "float32"
+HOP1_ENGINES = 4
+HOP2_ENGINES = 8
+
+SCRATCH = {
+    "kd": ("dram", [128, 128], BF), "vd": ("dram", [128, 128], BF),
+    "qs": ("sbuf", [128, 32], BF), "ks": ("sbuf", [128, 128], BF), "vs": ("sbuf", [128, 128], BF),
+    "kp": ("sbuf", [128, 128], BF), "vp": ("sbuf", [128, 128], BF),
+    "zm": ("sbuf", [128, 32], F32), "idn": ("sbuf", [128, 32], BF),
+    "m0": ("sbuf", [128, 32], F32), "da": ("sbuf", [128, 32], BF),
+    "col": ("sbuf", [128, 8], F32),
+    "po": ("sbuf", [128, 128], BF), "pp": ("sbuf", [128, 128], BF),
+    "pto": ("sbuf", [128, 32], BF), "ptp": ("sbuf", [128, 32], BF),
+    "oo": ("sbuf", [128, 128], BF), "ys": ("sbuf", [128, 128], BF),
+    "psa": ("psum", [128, 512], F32), "psb": ("psum", [128, 512], F32),
+    "psc": ("psum", [128, 1024], BF), "psd": ("psum", [128, 1024], BF),
+    "pse": ("psum", [128, 512], F32), "psf": ("psum", [128, 512], F32),
+}
+SEMAPHORES = ["kd", "vd", "ql", "kl", "vl", "ms", "zz", "idn", "sto", "nmo", "pl", "m0", "a0", "pto", "ptos", "oo", "oos",
+              "karr", "varr", "stp", "nm", "a1", "a2", "tp", "tps", "yy", "ll", "rr", "ys", "st", "loc"]
+
+NMO, LO, NM, LP, AL, LL, RI = range(7)
+
+
+def pick(mask, n):
+    bits = [b for b in range(mask.bit_length()) if (mask >> b) & 1]
+    step = len(bits) // n
+    return sum(1 << bits[i * step] for i in range(n))
+
+
+def helpers(T, topo, src, dst):
+    group = list(T.cores)
+    cand = [c for c in range(topo.CHIPS * topo.CORES_PER_CHIP)
+            if topo.chip(c) == topo.chip(src) and c not in group and topo.may_write(c, dst)]
+    near = [c for c in cand if topo.die(c) == topo.die(src)]
+    far = [c for c in cand if topo.die(c) != topo.die(src)]
+    return near[0], far[0]
+
+
+def send(g, topo, src, dst, out_ap, in_ap, remote_sem, local_sem, engines):
+    rid, pid, _ = topo.addr(dst)
+    g.remote_dma(out_ap=out_ap, in_ap=in_ap, remote_sem=remote_sem, local_sem=local_sem, pid=pid, routing_id=rid,
+                 dma_engine_mask=pick(topo.mask(src, dst), engines))
+
+
+def rank_program(g, core, T, topo):
+    S = T.sem
+    cores = list(T.cores)
+    rank = T.rank_of(core)
+
+    if rank is None:
+        for i in range(len(cores) - 1):
+            hk, hv = helpers(T, topo, cores[i], cores[i + 1])
+            for h, stage, land, sem in ((hk, T.kd, T.kp, S.karr), (hv, T.vd, T.vp, S.varr)):
+                if core == h:
+                    g.wait_ge(sem, HOP1_ENGINES)
+                    send(g, topo, core, cores[i + 1], land[:], stage[:], sem, S.loc, HOP2_ENGINES)
+                    g.wait_ge(S.loc, HOP2_ENGINES)
+        return
+
+    prev = rank > 0
+    nxt = rank + 1 < len(cores)
+    sy, sc, ve, te = g.sync, g.scalar, g.vector, g.tensor
+    Exp, Copy = ActivationFunctionType.Exp, ActivationFunctionType.Copy
+    X = AxisListType.X
+    Q = slice(0, 32)
+
+    def col(j):
+        return T.col[Q, j:j + 1]
+
+    if nxt:
+        sy.dma_start(out=T.kd[:], in_=T.k[:]).then_inc(S.kd, 16)
+        sc.dma_start(out=T.vd[:], in_=T.v[:]).then_inc(S.vd, 16)
+    sy.dma_start(out=T.qs[:], in_=T.q[:]).then_inc(S.ql, 16)
+    sy.dma_start(out=T.ks[:], in_=T.k[:]).then_inc(S.kl, 16)
+    sc.dma_start(out=T.vs[:], in_=T.v[:]).then_inc(S.vl, 16)
+
+    ve.memset(T.zm[Q, :], 0.0).then_inc(S.ms, 1)
+    g.wait_ge(S.ms, 1)
+    g.affine_select(out=T.zm[Q, :], in_=T.zm[Q, :], pattern=[[-1, 32]], compare_op=AluOpType.is_equal, fill=-30000.0,
+                    base=0, channel_multiplier=1).then_inc(S.zz, 1)
+    if nxt:
+        hk, hv = helpers(T, topo, core, cores[rank + 1])
+        g.wait_ge(S.kd, 16)
+        send(g, topo, core, hk, T.kd[:], T.kd[:], S.karr, S.loc, HOP1_ENGINES)
+        g.wait_ge(S.vd, 16)
+        send(g, topo, core, hv, T.vd[:], T.vd[:], S.varr, S.loc, HOP1_ENGINES)
+        g.wait_ge(S.loc, 2 * HOP1_ENGINES)
+
+    ve.wait_ge(S.zz, 1)
+    ve.tensor_scalar(out=T.idn[Q, :], in0=T.zm[Q, :], scalar1=0.0, scalar2=None, op0=AluOpType.is_equal).then_inc(S.idn, 1)
+
+    te.wait_ge(S.ql, 16)
+    te.wait_ge(S.kl, 16)
+    te.matmul(out=T.psa[Q, 0:128], lhsT=T.qs[:, :], rhs=T.ks[:, :], start=True, stop=True).then_inc(S.sto, 1)
+
+    ve.wait_ge(S.sto, 1)
+    ve.tensor_reduce(out=col(NMO), in_=T.psa[Q, 0:128], axis=X, op=AluOpType.max, negate=True).then_inc(S.nmo, 1)
+
+    sc.wait_ge(S.nmo, 1)
+    sc.activation(out=T.po[Q, :], in_=T.psa[Q, 0:128], func=Exp, bias=col(NMO), scale=1.0,
+                  accum_out=col(LO)).then_inc(S.a0, 1)
+
+    if prev:
+        ve.wait_ge(S.nmo, 1)
+        ve.tensor_scalar(out=T.psb[Q, 128:129], in0=col(NMO), scalar1=-1.0, scalar2=None,
+                         op0=AluOpType.mult).then_inc(S.pl, 1)
+        ve.tensor_scalar(out=T.m0[Q, :], in0=T.zm[Q, :], scalar1=col(NMO), scalar2=None,
+                         op0=AluOpType.subtract).then_inc(S.m0, 1)
+
+    te.wait_ge(S.a0, 1)
+    te.wait_ge(S.idn, 1)
+    te.transpose(out=T.psc[:, 0:32], in_=T.po[Q, :], identity=T.idn[Q, :]).then_inc(S.pto, 1)
+    ve.wait_ge(S.pto, 1)
+    ve.tensor_copy(out=T.pto[:, :], in_=T.psc[:, 0:32]).then_inc(S.ptos, 1)
+    te.wait_ge(S.ptos, 1)
+    te.wait_ge(S.vl, 16)
+    te.matmul(out=T.pse[Q, 0:128], lhsT=T.pto[:, :], rhs=T.vs[:, :], start=True, stop=True).then_inc(S.oo, 1)
+    ve.wait_ge(S.oo, 1)
+
+    if not prev:
+        ve.wait_ge(S.a0, 1)
+        ve.reciprocal(out=col(RI), in_=col(LO)).then_inc(S.rr, 1)
+        ve.wait_ge(S.rr, 1)
+        ve.tensor_scalar(out=T.ys[Q, :], in0=T.pse[Q, 0:128], scalar1=col(RI), scalar2=None,
+                         op0=AluOpType.mult).then_inc(S.ys, 1)
+    else:
+        ve.tensor_copy(out=T.oo[Q, :], in_=T.pse[Q, 0:128]).then_inc(S.oos, 1)
+
+        te.wait_ge(S.pl, 1)
+        te.wait_ge(S.karr, HOP2_ENGINES)
+        te.matmul(out=T.psb[Q, 0:128], lhsT=T.qs[:, :], rhs=T.kp[:, :], start=True, stop=True).then_inc(S.stp, 1)
+
+        ve.wait_ge(S.stp, 1)
+        ve.tensor_reduce(out=col(NM), in_=T.psb[Q, 0:129], axis=X, op=AluOpType.max, negate=True).then_inc(S.nm, 1)
+
+        sc.wait_ge(S.m0, 1)
+        sc.wait_ge(S.nm, 1)
+        sc.activation(out=T.da[Q, :], in_=T.m0[Q, :], func=Exp, bias=col(NM), scale=1.0,
+                      accum_out=col(AL)).then_inc(S.a2, 1)
+        sc.activation(out=T.pp[Q, :], in_=T.psb[Q, 0:128], func=Exp, bias=col(NM), scale=1.0,
+                      accum_out=col(LP)).then_inc(S.a1, 1)
+
+        te.wait_ge(S.oos, 1)
+        te.wait_ge(S.a2, 1)
+        te.matmul(out=T.psf[Q, 0:128], lhsT=T.da[Q, :], rhs=T.oo[Q, :], start=True, stop=False)
+        te.wait_ge(S.a1, 1)
+        te.transpose(out=T.psd[:, 0:32], in_=T.pp[Q, :], identity=T.idn[Q, :]).then_inc(S.tp, 1)
+        sc.wait_ge(S.tp, 1)
+        sc.activation(out=T.ptp[:, :], in_=T.psd[:, 0:32], func=Copy).then_inc(S.tps, 1)
+        te.wait_ge(S.tps, 1)
+        te.wait_ge(S.varr, HOP2_ENGINES)
+        te.matmul(out=T.psf[Q, 0:128], lhsT=T.ptp[:, :], rhs=T.vp[:, :], start=False, stop=True).then_inc(S.yy, 1)
+
+        ve.wait_ge(S.a2, 1)
+        ve.wait_ge(S.a1, 1)
+        ve.tensor_scalar(out=col(LL), in0=col(LO), scalar1=col(AL), scalar2=col(LP), op0=AluOpType.mult,
+                         op1=AluOpType.add).then_inc(S.ll, 1)
+        ve.wait_ge(S.ll, 1)
+        ve.reciprocal(out=col(RI), in_=col(LL)).then_inc(S.rr, 1)
+        ve.wait_ge(S.rr, 1)
+        ve.wait_ge(S.yy, 1)
+        ve.tensor_scalar(out=T.ys[Q, :], in0=T.psf[Q, 0:128], scalar1=col(RI), scalar2=None,
+                         op0=AluOpType.mult).then_inc(S.ys, 1)
+
+    sy.wait_ge(S.ys, 1)
+    sy.dma_start(out=T.y[:], in_=T.ys[Q, :]).then_inc(S.st, 16)
+    sy.wait_ge(S.st, 16)

@@ -19,7 +19,7 @@ SCRATCH = {
     "pse": ("psum", [128, 512], F32), "psf": ("psum", [128, 512], F32),
 }
 SEMAPHORES = ["kd", "vd", "ql", "kl", "vl", "ms", "zz", "idn", "sto", "nmo", "pl", "m0", "a0", "pto", "ptos", "oo", "oos",
-              "karr", "varr", "stp", "nm", "a1", "a2", "tp", "tps", "yy", "ll", "rr", "ys", "st", "loc"]
+              "cidn", "czm", "karr", "varr", "stp", "nm", "a1", "a2", "tp", "tps", "yy", "ll", "rr", "ys", "st", "loc"]
 
 NMO, LO, NM, LP, AL, LL, RI = range(7)
 
@@ -45,6 +45,18 @@ def send(g, topo, src, dst, out_ap, in_ap, remote_sem, local_sem, engines):
                  dma_engine_mask=pick(topo.mask(src, dst), engines))
 
 
+def constants(g, T, P, identity):
+    S = T.sem
+    g.vector.memset(T.zm[P, :], 0.0).then_inc(S.ms, 1)
+    g.wait_ge(S.ms, 1)
+    g.affine_select(out=T.zm[P, :], in_=T.zm[P, :], pattern=[[-1, 32]], compare_op=AluOpType.is_equal, fill=-30000.0,
+                    base=0, channel_multiplier=1).then_inc(S.zz, 1)
+    if identity:
+        g.vector.wait_ge(S.zz, 1)
+        g.vector.tensor_scalar(out=T.idn[P, :], in0=T.zm[P, :], scalar1=0.0, scalar2=None,
+                               op0=AluOpType.is_equal).then_inc(S.idn, 1)
+
+
 def rank_program(g, core, T, topo):
     S = T.sem
     cores = list(T.cores)
@@ -53,11 +65,18 @@ def rank_program(g, core, T, topo):
     if rank is None:
         for i in range(len(cores) - 1):
             hk, hv = helpers(T, topo, cores[i], cores[i + 1])
-            for h, stage, land, sem in ((hk, T.kd, T.kp, S.karr), (hv, T.vd, T.vp, S.varr)):
+            for h, ident, stage, land, sem in ((hk, True, T.kd, T.kp, S.karr), (hv, False, T.vd, T.vp, S.varr)):
                 if core == h:
+                    constants(g, T, slice(0, 128), ident)
+                    if ident:
+                        g.wait_ge(S.idn, 1)
+                        send(g, topo, core, cores[i + 1], T.idn[:], T.idn[:], S.cidn, S.loc, HOP2_ENGINES)
+                    else:
+                        g.wait_ge(S.zz, 1)
+                        send(g, topo, core, cores[i + 1], T.zm[:], T.zm[:], S.czm, S.loc, HOP2_ENGINES)
                     g.wait_ge(sem, HOP1_ENGINES)
                     send(g, topo, core, cores[i + 1], land[:], stage[:], sem, S.loc, HOP2_ENGINES)
-                    g.wait_ge(S.loc, HOP2_ENGINES)
+                    g.wait_ge(S.loc, 2 * HOP2_ENGINES)
         return
 
     prev = rank > 0
@@ -77,10 +96,8 @@ def rank_program(g, core, T, topo):
     sy.dma_start(out=T.ks[:], in_=T.k[:]).then_inc(S.kl, 16)
     sc.dma_start(out=T.vs[:], in_=T.v[:]).then_inc(S.vl, 16)
 
-    ve.memset(T.zm[Q, :], 0.0).then_inc(S.ms, 1)
-    g.wait_ge(S.ms, 1)
-    g.affine_select(out=T.zm[Q, :], in_=T.zm[Q, :], pattern=[[-1, 32]], compare_op=AluOpType.is_equal, fill=-30000.0,
-                    base=0, channel_multiplier=1).then_inc(S.zz, 1)
+    if not prev:
+        constants(g, T, Q, True)
     if nxt:
         hk, hv = helpers(T, topo, core, cores[rank + 1])
         g.wait_ge(S.kd, 16)
@@ -88,9 +105,6 @@ def rank_program(g, core, T, topo):
         g.wait_ge(S.vd, 16)
         send(g, topo, core, hv, T.vd[:], T.vd[:], S.varr, S.loc, HOP1_ENGINES)
         g.wait_ge(S.loc, 2 * HOP1_ENGINES)
-
-    ve.wait_ge(S.zz, 1)
-    ve.tensor_scalar(out=T.idn[Q, :], in0=T.zm[Q, :], scalar1=0.0, scalar2=None, op0=AluOpType.is_equal).then_inc(S.idn, 1)
 
     te.wait_ge(S.ql, 16)
     te.wait_ge(S.kl, 16)
@@ -107,11 +121,15 @@ def rank_program(g, core, T, topo):
         ve.wait_ge(S.nmo, 1)
         ve.tensor_scalar(out=T.psb[Q, 128:129], in0=col(NMO), scalar1=-1.0, scalar2=None,
                          op0=AluOpType.mult).then_inc(S.pl, 1)
+        ve.wait_ge(S.czm, HOP2_ENGINES)
         ve.tensor_scalar(out=T.m0[Q, :], in0=T.zm[Q, :], scalar1=col(NMO), scalar2=None,
                          op0=AluOpType.subtract).then_inc(S.m0, 1)
 
     te.wait_ge(S.a0, 1)
-    te.wait_ge(S.idn, 1)
+    if prev:
+        te.wait_ge(S.cidn, HOP2_ENGINES)
+    else:
+        te.wait_ge(S.idn, 1)
     te.transpose(out=T.psc[:, 0:32], in_=T.po[Q, :], identity=T.idn[Q, :]).then_inc(S.pto, 1)
     ve.wait_ge(S.pto, 1)
     ve.tensor_copy(out=T.pto[:, :], in_=T.psc[:, 0:32]).then_inc(S.ptos, 1)

@@ -1,25 +1,28 @@
 from concourse.mybir import AluOpType, AxisListType, ActivationFunctionType
 
 BF, F32 = "bfloat16", "float32"
-HOP1_ENGINES = 4
+HOP1_ENGINES = 8
 HOP2_ENGINES = 8
+K_PIECE, V_PIECE, R_PIECE = slice(0, 8), slice(8, 16), slice(16, 32)
 
 SCRATCH = {
     "kd": ("dram", [128, 128], BF), "vd": ("dram", [128, 128], BF),
     "qs": ("sbuf", [128, 32], BF), "ks": ("sbuf", [128, 128], BF), "vs": ("sbuf", [128, 128], BF),
     "kp": ("sbuf", [128, 128], BF), "vp": ("sbuf", [128, 128], BF),
-    "zm": ("sbuf", [128, 32], F32), "idn": ("sbuf", [128, 32], BF),
-    "m0": ("sbuf", [128, 32], F32), "da": ("sbuf", [128, 32], BF),
+    "dd": ("sbuf", [128, 32], F32), "sq": ("sbuf", [128, 32], F32), "idn": ("sbuf", [128, 32], BF),
+    "dz": ("sbuf", [128, 32], F32), "zq": ("sbuf", [128, 32], F32), "m0": ("sbuf", [128, 32], F32),
+    "da": ("sbuf", [128, 32], BF),
     "col": ("sbuf", [128, 8], F32),
     "po": ("sbuf", [128, 128], BF), "pp": ("sbuf", [128, 128], BF),
     "pto": ("sbuf", [128, 32], BF), "ptp": ("sbuf", [128, 32], BF),
     "oo": ("sbuf", [128, 128], BF), "ys": ("sbuf", [128, 128], BF),
     "psa": ("psum", [128, 512], F32), "psb": ("psum", [128, 512], F32),
     "psc": ("psum", [128, 1024], BF), "psd": ("psum", [128, 1024], BF),
-    "pse": ("psum", [128, 512], F32), "psf": ("psum", [128, 512], F32),
+    "pse": ("psum", [128, 512], F32), "psf": ("psum", [128, 512], F32), "psg": ("psum", [128, 512], F32),
 }
-SEMAPHORES = ["kd", "vd", "ql", "kl", "vl", "ms", "zz", "idn", "sto", "nmo", "pl", "m0", "a0", "pto", "ptos", "oo", "oos",
-              "cidn", "czm", "karr", "varr", "stp", "nm", "a1", "a2", "tp", "tps", "yy", "ll", "rr", "ys", "st", "loc"]
+SEMAPHORES = ["kd", "vd", "ql", "kl", "vl", "dif", "sqr", "idn", "sto", "nmo", "pl", "zq", "m0", "a0", "pto", "ptos", "oo",
+              "oos", "cdz", "karr", "varr", "stp", "nm", "a1", "a2", "tp", "tps", "yy", "yyb", "ll", "rr", "ys", "ysb", "st",
+              "loc"]
 
 NMO, LO, NM, LP, AL, LL, RI = range(7)
 
@@ -39,22 +42,35 @@ def helpers(T, topo, src, dst):
     return near[0], far[0]
 
 
-def send(g, topo, src, dst, out_ap, in_ap, remote_sem, local_sem, engines):
+def piece_peers(T, topo):
+    cores = list(T.cores)
+    n = len(cores)
+    to, seen = {}, []
+    for r in range(n):
+        if r in seen:
+            continue
+        cls = [s for s in range(n) if s == r or (topo.may_write(cores[r], cores[s]) and topo.may_write(cores[s], cores[r]))]
+        seen += cls
+        snd = [s for s in cls if s + 1 < n]
+        rcv = [s for s in cls if s > 0]
+        for shift in range(len(rcv)):
+            if all(snd[i] != rcv[(i + shift) % len(rcv)] for i in range(len(snd))):
+                for i in range(len(snd)):
+                    to[snd[i]] = rcv[(i + shift) % len(rcv)]
+                break
+    return to
+
+
+def send(g, topo, src, dst, out_ap, in_ap, remote_sem, local_sem, engines, within=None):
     rid, pid, _ = topo.addr(dst)
+    allowed = topo.mask(src, dst) if within is None else topo.mask(src, dst) & within
     g.remote_dma(out_ap=out_ap, in_ap=in_ap, remote_sem=remote_sem, local_sem=local_sem, pid=pid, routing_id=rid,
-                 dma_engine_mask=pick(topo.mask(src, dst), engines))
+                 dma_engine_mask=pick(allowed, engines))
 
 
-def constants(g, T, P, identity):
-    S = T.sem
-    g.vector.memset(T.zm[P, :], 0.0).then_inc(S.ms, 1)
-    g.wait_ge(S.ms, 1)
-    g.affine_select(out=T.zm[P, :], in_=T.zm[P, :], pattern=[[-1, 32]], compare_op=AluOpType.is_equal, fill=-30000.0,
-                    base=0, channel_multiplier=1).then_inc(S.zz, 1)
-    if identity:
-        g.vector.wait_ge(S.zz, 1)
-        g.vector.tensor_scalar(out=T.idn[P, :], in0=T.zm[P, :], scalar1=0.0, scalar2=None,
-                               op0=AluOpType.is_equal).then_inc(S.idn, 1)
+def differences(g, T):
+    g.iota(T.dd[:], pattern=[[-1, 32]], base=0, channel_multiplier=1,
+           allow_small_or_imprecise_dtypes=True).then_inc(T.sem.dif, 1)
 
 
 def rank_program(g, core, T, topo):
@@ -65,15 +81,11 @@ def rank_program(g, core, T, topo):
     if rank is None:
         for i in range(len(cores) - 1):
             hk, hv = helpers(T, topo, cores[i], cores[i + 1])
-            for h, ident, stage, land, sem in ((hk, True, T.kd, T.kp, S.karr), (hv, False, T.vd, T.vp, S.varr)):
+            for h, piece, stage, land, sem in ((hk, K_PIECE, T.kd, T.kp, S.karr), (hv, V_PIECE, T.vd, T.vp, S.varr)):
                 if core == h:
-                    constants(g, T, slice(0, 128), ident)
-                    if ident:
-                        g.wait_ge(S.idn, 1)
-                        send(g, topo, core, cores[i + 1], T.idn[:], T.idn[:], S.cidn, S.loc, HOP2_ENGINES)
-                    else:
-                        g.wait_ge(S.zz, 1)
-                        send(g, topo, core, cores[i + 1], T.zm[:], T.zm[:], S.czm, S.loc, HOP2_ENGINES)
+                    differences(g, T)
+                    g.wait_ge(S.dif, 1)
+                    send(g, topo, core, cores[i + 1], T.dz[:, piece], T.dd[:, piece], S.cdz, S.loc, HOP2_ENGINES)
                     g.wait_ge(sem, HOP1_ENGINES)
                     send(g, topo, core, cores[i + 1], land[:], stage[:], sem, S.loc, HOP2_ENGINES)
                     g.wait_ge(S.loc, 2 * HOP2_ENGINES)
@@ -82,7 +94,7 @@ def rank_program(g, core, T, topo):
     prev = rank > 0
     nxt = rank + 1 < len(cores)
     sy, sc, ve, te = g.sync, g.scalar, g.vector, g.tensor
-    Exp, Copy = ActivationFunctionType.Exp, ActivationFunctionType.Copy
+    Exp, Copy, Square = ActivationFunctionType.Exp, ActivationFunctionType.Copy, ActivationFunctionType.Square
     X = AxisListType.X
     Q = slice(0, 32)
 
@@ -92,19 +104,27 @@ def rank_program(g, core, T, topo):
     if nxt:
         sy.dma_start(out=T.kd[:], in_=T.k[:]).then_inc(S.kd, 16)
         sc.dma_start(out=T.vd[:], in_=T.v[:]).then_inc(S.vd, 16)
-    sy.dma_start(out=T.qs[:], in_=T.q[:]).then_inc(S.ql, 16)
     sy.dma_start(out=T.ks[:], in_=T.k[:]).then_inc(S.kl, 16)
-    sc.dma_start(out=T.vs[:], in_=T.v[:]).then_inc(S.vl, 16)
+    sc.dma_start(out=T.qs[:], in_=T.q[:]).then_inc(S.ql, 16)
+    sy.dma_start(out=T.vs[:], in_=T.v[:]).then_inc(S.vl, 16)
 
-    if not prev:
-        constants(g, T, Q, True)
+    differences(g, T)
     if nxt:
+        peer = cores[piece_peers(T, topo)[rank]]
         hk, hv = helpers(T, topo, core, cores[rank + 1])
+        same = topo.mask(core, peer)
+        g.wait_ge(S.dif, 1)
+        send(g, topo, core, peer, T.dz[:, R_PIECE], T.dd[:, R_PIECE], S.cdz, S.loc, HOP1_ENGINES)
         g.wait_ge(S.kd, 16)
-        send(g, topo, core, hk, T.kd[:], T.kd[:], S.karr, S.loc, HOP1_ENGINES)
+        send(g, topo, core, hk, T.kd[:], T.kd[:], S.karr, S.loc, HOP1_ENGINES, same)
         g.wait_ge(S.vd, 16)
-        send(g, topo, core, hv, T.vd[:], T.vd[:], S.varr, S.loc, HOP1_ENGINES)
-        g.wait_ge(S.loc, 2 * HOP1_ENGINES)
+        send(g, topo, core, hv, T.vd[:], T.vd[:], S.varr, S.loc, HOP1_ENGINES, same)
+        g.wait_ge(S.loc, 3 * HOP1_ENGINES)
+
+    sc.wait_ge(S.dif, 1)
+    sc.activation(out=T.sq[Q, :], in_=T.dd[Q, :], func=Square).then_inc(S.sqr, 1)
+    sc.wait_ge(S.sqr, 1)
+    sc.activation(out=T.idn[Q, :], in_=T.sq[Q, :], func=Exp, scale=-30000.0).then_inc(S.idn, 1)
 
     te.wait_ge(S.ql, 16)
     te.wait_ge(S.kl, 16)
@@ -121,15 +141,9 @@ def rank_program(g, core, T, topo):
         ve.wait_ge(S.nmo, 1)
         ve.tensor_scalar(out=T.psb[Q, 128:129], in0=col(NMO), scalar1=-1.0, scalar2=None,
                          op0=AluOpType.mult).then_inc(S.pl, 1)
-        ve.wait_ge(S.czm, HOP2_ENGINES)
-        ve.tensor_scalar(out=T.m0[Q, :], in0=T.zm[Q, :], scalar1=col(NMO), scalar2=None,
-                         op0=AluOpType.subtract).then_inc(S.m0, 1)
 
     te.wait_ge(S.a0, 1)
-    if prev:
-        te.wait_ge(S.cidn, HOP2_ENGINES)
-    else:
-        te.wait_ge(S.idn, 1)
+    te.wait_ge(S.idn, 1)
     te.transpose(out=T.psc[:, 0:32], in_=T.po[Q, :], identity=T.idn[Q, :]).then_inc(S.pto, 1)
     ve.wait_ge(S.pto, 1)
     ve.tensor_copy(out=T.pto[:, :], in_=T.psc[:, 0:32]).then_inc(S.ptos, 1)
@@ -146,6 +160,11 @@ def rank_program(g, core, T, topo):
                          op0=AluOpType.mult).then_inc(S.ys, 1)
     else:
         ve.tensor_copy(out=T.oo[Q, :], in_=T.pse[Q, 0:128]).then_inc(S.oos, 1)
+        ve.wait_ge(S.cdz, 2 * HOP2_ENGINES + HOP1_ENGINES)
+        ve.tensor_tensor(out=T.zq[Q, :], in0=T.dz[Q, :], in1=T.dz[Q, :], op=AluOpType.mult).then_inc(S.zq, 1)
+        ve.wait_ge(S.zq, 1)
+        ve.tensor_scalar(out=T.m0[Q, :], in0=T.zq[Q, :], scalar1=-30000.0, scalar2=col(NMO), op0=AluOpType.mult,
+                         op1=AluOpType.subtract).then_inc(S.m0, 1)
 
         te.wait_ge(S.pl, 1)
         te.wait_ge(S.karr, HOP2_ENGINES)
@@ -163,14 +182,16 @@ def rank_program(g, core, T, topo):
 
         te.wait_ge(S.oos, 1)
         te.wait_ge(S.a2, 1)
-        te.matmul(out=T.psf[Q, 0:128], lhsT=T.da[Q, :], rhs=T.oo[Q, :], start=True, stop=False)
+        te.matmul(out=T.psf[Q, 0:64], lhsT=T.da[Q, :], rhs=T.oo[Q, 0:64], start=True, stop=False)
+        te.matmul(out=T.psg[Q, 0:64], lhsT=T.da[Q, :], rhs=T.oo[Q, 64:128], start=True, stop=False)
         te.wait_ge(S.a1, 1)
         te.transpose(out=T.psd[:, 0:32], in_=T.pp[Q, :], identity=T.idn[Q, :]).then_inc(S.tp, 1)
         sc.wait_ge(S.tp, 1)
         sc.activation(out=T.ptp[:, :], in_=T.psd[:, 0:32], func=Copy).then_inc(S.tps, 1)
         te.wait_ge(S.tps, 1)
         te.wait_ge(S.varr, HOP2_ENGINES)
-        te.matmul(out=T.psf[Q, 0:128], lhsT=T.ptp[:, :], rhs=T.vp[:, :], start=False, stop=True).then_inc(S.yy, 1)
+        te.matmul(out=T.psf[Q, 0:64], lhsT=T.ptp[:, :], rhs=T.vp[:, 0:64], start=False, stop=True).then_inc(S.yy, 1)
+        te.matmul(out=T.psg[Q, 0:64], lhsT=T.ptp[:, :], rhs=T.vp[:, 64:128], start=False, stop=True).then_inc(S.yyb, 1)
 
         ve.wait_ge(S.a2, 1)
         ve.wait_ge(S.a1, 1)
@@ -180,9 +201,14 @@ def rank_program(g, core, T, topo):
         ve.reciprocal(out=col(RI), in_=col(LL)).then_inc(S.rr, 1)
         ve.wait_ge(S.rr, 1)
         ve.wait_ge(S.yy, 1)
-        ve.tensor_scalar(out=T.ys[Q, :], in0=T.psf[Q, 0:128], scalar1=col(RI), scalar2=None,
+        ve.tensor_scalar(out=T.ys[Q, 0:64], in0=T.psf[Q, 0:64], scalar1=col(RI), scalar2=None,
                          op0=AluOpType.mult).then_inc(S.ys, 1)
+        sc.wait_ge(S.rr, 1)
+        sc.wait_ge(S.yyb, 1)
+        sc.activation(out=T.ys[Q, 64:128], in_=T.psg[Q, 0:64], func=Copy, scale=col(RI)).then_inc(S.ysb, 1)
 
     sy.wait_ge(S.ys, 1)
+    if prev:
+        sy.wait_ge(S.ysb, 1)
     sy.dma_start(out=T.y[:], in_=T.ys[Q, :]).then_inc(S.st, 16)
     sy.wait_ge(S.st, 16)

from concourse.mybir import AluOpType, AxisListType, ActivationFunctionType

BF, F32 = "bfloat16", "float32"
HOP1_ENGINES = 8
HOP2_ENGINES = 8
K_PIECE, V_PIECE, R_PIECE = slice(0, 8), slice(8, 16), slice(16, 32)

SCRATCH = {
    "kd": ("dram", [128, 128], BF), "vd": ("dram", [128, 128], BF),
    "qs": ("sbuf", [128, 32], BF), "ks": ("sbuf", [128, 128], BF), "vs": ("sbuf", [128, 128], BF),
    "kp": ("sbuf", [128, 128], BF), "vp": ("sbuf", [128, 128], BF),
    "dd": ("sbuf", [128, 32], F32), "sq": ("sbuf", [128, 32], F32), "idn": ("sbuf", [128, 32], BF),
    "dz": ("sbuf", [128, 32], F32), "zq": ("sbuf", [128, 32], F32), "m0": ("sbuf", [128, 32], F32),
    "da": ("sbuf", [128, 32], BF),
    "col": ("sbuf", [128, 8], F32),
    "po": ("sbuf", [128, 128], BF), "pp": ("sbuf", [128, 128], BF),
    "pto": ("sbuf", [128, 32], BF), "ptp": ("sbuf", [128, 32], BF),
    "oo": ("sbuf", [128, 128], BF), "ys": ("sbuf", [128, 128], BF),
    "psa": ("psum", [128, 512], F32), "psb": ("psum", [128, 512], F32),
    "psc": ("psum", [128, 1024], BF), "psd": ("psum", [128, 1024], BF),
    "pse": ("psum", [128, 512], F32), "psf": ("psum", [128, 512], F32), "psg": ("psum", [128, 512], F32),
}
SEMAPHORES = ["kd", "vd", "ql", "kl", "vl", "dif", "sqr", "idn", "sto", "nmo", "pl", "zq", "m0", "a0", "pto", "ptos", "oo",
              "oos", "cdz", "karr", "varr", "stp", "nm", "a1", "a2", "tp", "tps", "yy", "yyb", "ll", "rr", "ys", "ysb", "st",
              "loc"]

NMO, LO, NM, LP, AL, LL, RI = range(7)


def pick(mask, n):
    bits = [b for b in range(mask.bit_length()) if (mask >> b) & 1]
    step = len(bits) // n
    return sum(1 << bits[i * step] for i in range(n))


def helpers(T, topo, src, dst):
    group = list(T.cores)
    cand = [c for c in range(topo.CHIPS * topo.CORES_PER_CHIP)
            if topo.chip(c) == topo.chip(src) and c not in group and topo.may_write(c, dst)]
    near = [c for c in cand if topo.die(c) == topo.die(src)]
    far = [c for c in cand if topo.die(c) != topo.die(src)]
    return near[0], far[0]


def piece_peers(T, topo):
    cores = list(T.cores)
    n = len(cores)
    to, seen = {}, []
    for r in range(n):
        if r in seen:
            continue
        cls = [s for s in range(n) if s == r or (topo.may_write(cores[r], cores[s]) and topo.may_write(cores[s], cores[r]))]
        seen += cls
        snd = [s for s in cls if s + 1 < n]
        rcv = [s for s in cls if s > 0]
        for shift in range(len(rcv)):
            if all(snd[i] != rcv[(i + shift) % len(rcv)] for i in range(len(snd))):
                for i in range(len(snd)):
                    to[snd[i]] = rcv[(i + shift) % len(rcv)]
                break
    return to


def send(g, topo, src, dst, out_ap, in_ap, remote_sem, local_sem, engines, within=None):
    rid, pid, _ = topo.addr(dst)
    allowed = topo.mask(src, dst) if within is None else topo.mask(src, dst) & within
    g.remote_dma(out_ap=out_ap, in_ap=in_ap, remote_sem=remote_sem, local_sem=local_sem, pid=pid, routing_id=rid,
                 dma_engine_mask=pick(allowed, engines))


def differences(g, T):
    g.iota(T.dd[:], pattern=[[-1, 32]], base=0, channel_multiplier=1,
           allow_small_or_imprecise_dtypes=True).then_inc(T.sem.dif, 1)


def rank_program(g, core, T, topo):
    S = T.sem
    cores = list(T.cores)
    rank = T.rank_of(core)

    if rank is None:
        for i in range(len(cores) - 1):
            hk, hv = helpers(T, topo, cores[i], cores[i + 1])
            for h, piece, stage, land, sem in ((hk, K_PIECE, T.kd, T.kp, S.karr), (hv, V_PIECE, T.vd, T.vp, S.varr)):
                if core == h:
                    differences(g, T)
                    g.wait_ge(S.dif, 1)
                    send(g, topo, core, cores[i + 1], T.dz[:, piece], T.dd[:, piece], S.cdz, S.loc, HOP2_ENGINES)
                    g.wait_ge(sem, HOP1_ENGINES)
                    send(g, topo, core, cores[i + 1], land[:], stage[:], sem, S.loc, HOP2_ENGINES)
                    g.wait_ge(S.loc, 2 * HOP2_ENGINES)
        return

    prev = rank > 0
    nxt = rank + 1 < len(cores)
    sy, sc, ve, te = g.sync, g.scalar, g.vector, g.tensor
    Exp, Copy, Square = ActivationFunctionType.Exp, ActivationFunctionType.Copy, ActivationFunctionType.Square
    X = AxisListType.X
    Q = slice(0, 32)

    def col(j):
        return T.col[Q, j:j + 1]

    if nxt:
        sy.dma_start(out=T.kd[:], in_=T.k[:]).then_inc(S.kd, 16)
        sc.dma_start(out=T.vd[:], in_=T.v[:]).then_inc(S.vd, 16)
    sy.dma_start(out=T.ks[:], in_=T.k[:]).then_inc(S.kl, 16)
    sc.dma_start(out=T.qs[:], in_=T.q[:]).then_inc(S.ql, 16)
    sy.dma_start(out=T.vs[:], in_=T.v[:]).then_inc(S.vl, 16)

    differences(g, T)
    if nxt:
        peer = cores[piece_peers(T, topo)[rank]]
        hk, hv = helpers(T, topo, core, cores[rank + 1])
        same = topo.mask(core, peer)
        g.wait_ge(S.dif, 1)
        send(g, topo, core, peer, T.dz[:, R_PIECE], T.dd[:, R_PIECE], S.cdz, S.loc, HOP1_ENGINES)
        g.wait_ge(S.kd, 16)
        send(g, topo, core, hk, T.kd[:], T.kd[:], S.karr, S.loc, HOP1_ENGINES, same)
        g.wait_ge(S.vd, 16)
        send(g, topo, core, hv, T.vd[:], T.vd[:], S.varr, S.loc, HOP1_ENGINES, same)
        g.wait_ge(S.loc, 3 * HOP1_ENGINES)

    sc.wait_ge(S.dif, 1)
    sc.activation(out=T.sq[Q, :], in_=T.dd[Q, :], func=Square).then_inc(S.sqr, 1)
    sc.wait_ge(S.sqr, 1)
    sc.activation(out=T.idn[Q, :], in_=T.sq[Q, :], func=Exp, scale=-30000.0).then_inc(S.idn, 1)

    te.wait_ge(S.ql, 16)
    te.wait_ge(S.kl, 16)
    te.matmul(out=T.psa[Q, 0:128], lhsT=T.qs[:, :], rhs=T.ks[:, :], start=True, stop=True).then_inc(S.sto, 1)

    ve.wait_ge(S.sto, 1)
    ve.tensor_reduce(out=col(NMO), in_=T.psa[Q, 0:128], axis=X, op=AluOpType.max, negate=True).then_inc(S.nmo, 1)

    sc.wait_ge(S.nmo, 1)
    sc.activation(out=T.po[Q, :], in_=T.psa[Q, 0:128], func=Exp, bias=col(NMO), scale=1.0,
                  accum_out=col(LO)).then_inc(S.a0, 1)

    if prev:
        ve.wait_ge(S.nmo, 1)
        ve.tensor_scalar(out=T.psb[Q, 128:129], in0=col(NMO), scalar1=-1.0, scalar2=None,
                         op0=AluOpType.mult).then_inc(S.pl, 1)

    te.wait_ge(S.a0, 1)
    te.wait_ge(S.idn, 1)
    te.transpose(out=T.psc[:, 0:32], in_=T.po[Q, :], identity=T.idn[Q, :]).then_inc(S.pto, 1)
    ve.wait_ge(S.pto, 1)
    ve.tensor_copy(out=T.pto[:, :], in_=T.psc[:, 0:32]).then_inc(S.ptos, 1)
    te.wait_ge(S.ptos, 1)
    te.wait_ge(S.vl, 16)
    te.matmul(out=T.pse[Q, 0:128], lhsT=T.pto[:, :], rhs=T.vs[:, :], start=True, stop=True).then_inc(S.oo, 1)
    ve.wait_ge(S.oo, 1)

    if not prev:
        ve.wait_ge(S.a0, 1)
        ve.reciprocal(out=col(RI), in_=col(LO)).then_inc(S.rr, 1)
        ve.wait_ge(S.rr, 1)
        ve.tensor_scalar(out=T.ys[Q, :], in0=T.pse[Q, 0:128], scalar1=col(RI), scalar2=None,
                         op0=AluOpType.mult).then_inc(S.ys, 1)
    else:
        ve.tensor_copy(out=T.oo[Q, :], in_=T.pse[Q, 0:128]).then_inc(S.oos, 1)
        ve.wait_ge(S.cdz, 2 * HOP2_ENGINES + HOP1_ENGINES)
        ve.tensor_tensor(out=T.zq[Q, :], in0=T.dz[Q, :], in1=T.dz[Q, :], op=AluOpType.mult).then_inc(S.zq, 1)
        ve.wait_ge(S.zq, 1)
        ve.tensor_scalar(out=T.m0[Q, :], in0=T.zq[Q, :], scalar1=-30000.0, scalar2=col(NMO), op0=AluOpType.mult,
                         op1=AluOpType.subtract).then_inc(S.m0, 1)

        te.wait_ge(S.pl, 1)
        te.wait_ge(S.karr, HOP2_ENGINES)
        te.matmul(out=T.psb[Q, 0:128], lhsT=T.qs[:, :], rhs=T.kp[:, :], start=True, stop=True).then_inc(S.stp, 1)

        ve.wait_ge(S.stp, 1)
        ve.tensor_reduce(out=col(NM), in_=T.psb[Q, 0:129], axis=X, op=AluOpType.max, negate=True).then_inc(S.nm, 1)

        sc.wait_ge(S.m0, 1)
        sc.wait_ge(S.nm, 1)
        sc.activation(out=T.da[Q, :], in_=T.m0[Q, :], func=Exp, bias=col(NM), scale=1.0,
                      accum_out=col(AL)).then_inc(S.a2, 1)
        sc.activation(out=T.pp[Q, :], in_=T.psb[Q, 0:128], func=Exp, bias=col(NM), scale=1.0,
                      accum_out=col(LP)).then_inc(S.a1, 1)

        te.wait_ge(S.oos, 1)
        te.wait_ge(S.a2, 1)
        te.matmul(out=T.psf[Q, 0:64], lhsT=T.da[Q, :], rhs=T.oo[Q, 0:64], start=True, stop=False)
        te.matmul(out=T.psg[Q, 0:64], lhsT=T.da[Q, :], rhs=T.oo[Q, 64:128], start=True, stop=False)
        te.wait_ge(S.a1, 1)
        te.transpose(out=T.psd[:, 0:32], in_=T.pp[Q, :], identity=T.idn[Q, :]).then_inc(S.tp, 1)
        sc.wait_ge(S.tp, 1)
        sc.activation(out=T.ptp[:, :], in_=T.psd[:, 0:32], func=Copy).then_inc(S.tps, 1)
        te.wait_ge(S.tps, 1)
        te.wait_ge(S.varr, HOP2_ENGINES)
        te.matmul(out=T.psf[Q, 0:64], lhsT=T.ptp[:, :], rhs=T.vp[:, 0:64], start=False, stop=True).then_inc(S.yy, 1)
        te.matmul(out=T.psg[Q, 0:64], lhsT=T.ptp[:, :], rhs=T.vp[:, 64:128], start=False, stop=True).then_inc(S.yyb, 1)

        ve.wait_ge(S.a2, 1)
        ve.wait_ge(S.a1, 1)
        ve.tensor_scalar(out=col(LL), in0=col(LO), scalar1=col(AL), scalar2=col(LP), op0=AluOpType.mult,
                         op1=AluOpType.add).then_inc(S.ll, 1)
        ve.wait_ge(S.ll, 1)
        ve.reciprocal(out=col(RI), in_=col(LL)).then_inc(S.rr, 1)
        ve.wait_ge(S.rr, 1)
        ve.wait_ge(S.yy, 1)
        ve.tensor_scalar(out=T.ys[Q, 0:64], in0=T.psf[Q, 0:64], scalar1=col(RI), scalar2=None,
                         op0=AluOpType.mult).then_inc(S.ys, 1)
        sc.wait_ge(S.rr, 1)
        sc.wait_ge(S.yyb, 1)
        sc.activation(out=T.ys[Q, 64:128], in_=T.psg[Q, 0:64], func=Copy, scale=col(RI)).then_inc(S.ysb, 1)

    sy.wait_ge(S.ys, 1)
    if prev:
        sy.wait_ge(S.ysb, 1)
    sy.dma_start(out=T.y[:], in_=T.ys[Q, :]).then_inc(S.st, 16)
    sy.wait_ge(S.st, 16)
